import numpy as np, ml_dtypes
CORES = [122,123,126,250,251,254,378,379,382,506,507,510]
N = 12
TK = 128
def setup_inputs(rng):
    return {"x": rng.standard_normal((N, 128, TK), dtype=np.float32).astype(ml_dtypes.bfloat16), "w": rng.standard_normal((N, 128, 128), dtype=np.float32).astype(ml_dtypes.bfloat16)}
def setup_inputs_big(rng):
    d = setup_inputs(rng)
    for k in ("x", "w"): d[k] = (d[k].astype(np.float32) * 1024.0).astype(d[k].dtype)
    return d
def setup_inputs_small(rng):
    d = setup_inputs(rng)
    for k in ("x", "w"): d[k] = (d[k].astype(np.float32) * (1 / 1024.0)).astype(d[k].dtype)
    return d
def setup_inputs_apart(rng):
    d = setup_inputs(rng)
    f = (10.0 ** rng.permutation(np.linspace(-1.5, 1.5, N))).astype(np.float32).reshape(N, 1, 1)
    for k in ("x", "w"): d[k] = (d[k].astype(np.float32) * f).astype(d[k].dtype)
    return d
def setup_inputs_neg(rng):
    d = setup_inputs(rng)
    d["x"] = (np.abs(d["x"].astype(np.float32)) * 1048576.0).astype(d["x"].dtype); d["w"] = (-np.abs(d["w"].astype(np.float32))).astype(d["w"].dtype)
    return d
def reference(x, w):
    X, W = x.astype(np.float64), w.astype(np.float64)
    y = np.stack([np.max([W[j].T @ X[r] for j in range(N)], axis=0) for r in range(N)])
    return {"y": y.astype(ml_dtypes.bfloat16)}

@@ -1,0 +1,147 @@
+from concourse.bass import DstId, RemoteDMATransfer
+from concourse.mybir import AluOpType
+
+D = 128
+
+SCRATCH = {
+    "wo": ("sbuf", [128, D], "bfloat16"),
+    "xo": ("sbuf", [128, D], "bfloat16"),
+    "wc": ("sbuf", [128, 2 * D], "bfloat16"),
+    "wf": ("sbuf", [128, 3 * D], "bfloat16"),
+    "xq": ("sbuf", [128, D], "bfloat16"),
+    "ao": ("sbuf", [128, D], "bfloat16"),
+    "aq": ("sbuf", [128, D], "bfloat16"),
+    "rs": ("sbuf", [128, D], "bfloat16"),
+    "yb": ("sbuf", [128, D], "bfloat16"),
+}
+for _b in range(8):
+    SCRATCH["p%d" % _b] = ("psum", [128, 512], "float32")
+
+SEMAPHORES = ["ld", "cw", "xa", "f0", "f1", "f2", "ra", "snd", "vs", "qd", "yd", "st"] + ["m%d" % _b for _b in range(8)]
+
+
+def _engines(mask):
+    return [e for e in range(mask.bit_length()) if (mask >> e) & 1]
+
+
+def _bits(engines):
+    return sum(1 << e for e in engines)
+
+
+def rank_program(g, core, T, topo):
+    if T.rank_of(core) is None:
+        return
+    S = T.sem
+    ranks = list(T.cores)
+
+    def chipset(c):
+        return [d for d in ranks if topo.host(d) == topo.host(c) and topo.chip(d) == topo.chip(c)]
+
+    def pos(c):
+        return chipset(c).index(c)
+
+    def crowded(c):
+        return len([d for d in chipset(c) if topo.die(d) == topo.die(c)]) > 1
+
+    def by_switch(c):
+        return [d for d in ranks if topo.same_plane(c, d)]
+
+    def by_cable(c):
+        return [d for d in ranks if topo.rack(topo.host(d)) != topo.rack(topo.host(c)) and topo.may_write(c, d)]
+
+    def w_givers(c):
+        return by_cable(c) if crowded(c) else by_switch(c)
+
+    def partner(c):
+        return [d for d in (by_switch(c) if crowded(c) else by_cable(c)) if pos(d) == pos(c)][0]
+
+    def transfer(dst_core, engines, sem, src, dst):
+        rid, pid = topo.addr(dst_core, core)
+        return RemoteDMATransfer(dst_ids=[DstId(rid=rid, pnc=pid)], dma_engine_mask=_bits(engines), remote_sem=sem,
+                                 src=src, dst=dst)
+
+    mate = partner(core)
+    near = [d for d in chipset(core) if d != core]
+    off = _engines(topo.mask(core, mate))
+    rest = [e for e in _engines(topo.mask(core, near[0])) if e not in off]
+
+    g.sync.dma_start(T.wo[:], T.w[:]).then_inc(S.ld, 16)
+    g.scalar.dma_start(T.xo[:], T.x[:]).then_inc(S.ld, 16)
+
+    far = []
+    for group in (by_switch(core), by_cable(core)):
+        for d in group:
+            if core in w_givers(d):
+                far.append((d, S["f%d" % pos(core)], T.wo[:], T.wf[:, pos(core) * D:(pos(core) + 1) * D]))
+            if d == mate:
+                far.append((d, S.xa, T.xo[:], T.xq[:]))
+    per = len(off) // len(far)
+    lanes = off[0::2] + off[1::2]
+    g.wait_ge(S.ld, 32)
+    g.remote_dma_fused([transfer(d, lanes[i * per:(i + 1) * per], sem, src, dst)
+                        for i, (d, sem, src, dst) in enumerate(far)], local_sem=S.snd)
+    near_sorted = sorted(near, key=lambda d: topo.die(d) == topo.die(core))
+    nper = len(rest) // len(near)
+    nlanes = rest[0::2] + rest[1::2]
+    calls = []
+    for i, d in enumerate(near_sorted):
+        slot = [e for e in chipset(d) if e != d].index(core)
+        calls.append(transfer(d, nlanes[i * nper:(i + 1) * nper], S.cw, T.wo[:], T.wc[:, slot * D:(slot + 1) * D]))
+    g.remote_dma_fused(calls, local_sem=S.snd)
+
+    te = g.tensor
+    home = [T.wo[:], T.wc[:, 0:D], T.wc[:, D:2 * D]]
+    order = [pos(d) for d in sorted(w_givers(core), key=lambda d: (crowded(d), pos(d)))]
+    te.wait_ge(S.ld, 32)
+    te.matmul(T.p0[:, 0:D], home[0], T.xo[:], True, True).then_inc(S.m0, 1)
+    te.wait_ge(S.cw, nper * len(near))
+    for k in (1, 2):
+        te.matmul(T.p0[:, k * D:(k + 1) * D], home[k], T.xo[:], True, True).then_inc(S.m0, 1)
+    te.wait_ge(S.xa, per)
+    for k in range(3):
+        te.matmul(T["p%d" % (1 + k)][:, 0:D], home[k], T.xq[:], True, True).then_inc(S["m%d" % (1 + k)], 1)
+    for k, j in enumerate(order):
+        te.wait_ge(S["f%d" % j], per)
+        te.matmul(T["p%d" % (4 + k)][:, 0:D], T.wf[:, j * D:(j + 1) * D], T.xq[:], True, True).then_inc(S["m%d" % (4 + k)], 1)
+    for k, j in enumerate(order):
+        te.matmul(T.p7[:, k * D:(k + 1) * D], T.wf[:, j * D:(j + 1) * D], T.xo[:], True, True).then_inc(S.m7, 1)
+
+    ve = g.vector
+    n = 0
+    ve.wait_ge(S.m0, 3)
+    ve.tensor_copy(T.ao[:], T.p0[:, 0:D]).then_inc(S.vs, 1)
+    n += 1
+    for k in (1, 2):
+        ve.wait_ge(S.vs, n)
+        ve.tensor_tensor(T.ao[:], T.ao[:], T.p0[:, k * D:(k + 1) * D], AluOpType.max).then_inc(S.vs, 1)
+        n += 1
+    ve.wait_ge(S.m1, 1)
+    ve.tensor_copy(T.aq[:], T.p1[:, 0:D]).then_inc(S.vs, 1)
+    n += 1
+    for b in range(2, 7):
+        ve.wait_ge(S["m%d" % b], 1)
+        ve.wait_ge(S.vs, n)
+        op = ve.tensor_tensor(T.aq[:], T.aq[:], T["p%d" % b][:, 0:D], AluOpType.max)
+        if b < 6:
+            op.then_inc(S.vs, 1)
+            n += 1
+        else:
+            op.then_inc(S.qd, 1)
+    ve.wait_ge(S.m7, 3)
+    for k in range(3):
+        ve.wait_ge(S.vs, n)
+        out = T.ao[:] if k < 2 else T.p0[:, 0:D]
+        ve.tensor_tensor(out, T.ao[:], T.p7[:, k * D:(k + 1) * D], AluOpType.max).then_inc(S.vs, 1)
+        n += 1
+    ve.wait_ge(S.ra, len(off))
+    ve.wait_ge(S.vs, n)
+    ve.tensor_tensor(T.yb[:], T.rs[:], T.p0[:, 0:D], AluOpType.max).then_inc(S.yd, 1)
+
+    rid, pid = topo.addr(mate, core)
+    g.wait_ge(S.qd, 1)
+    g.remote_dma(T.rs[:], T.aq[:], S.ra, S.snd, pid, rid, _bits(off))
+
+    g.sync.wait_ge(S.yd, 1)
+    g.sync.dma_start(T.y[:], T.yb[:]).then_inc(S.st, 16)
+    g.sync.wait_ge(S.st, 16)
+    g.wait_ge(S.snd, per * len(far) + nper * len(near) + len(off))

@@ -40,8 +40,11 @@ def rank_program(g, core, T, topo):
     def pos(c):
         return chipset(c).index(c)
 
-    def crowded(c):
-        return len([d for d in chipset(c) if topo.die(d) == topo.die(c)]) > 1
+    def diemates(c):
+        return [d for d in chipset(c) if topo.die(d) == topo.die(c)]
+
+    def cable_fed(c):
+        return len(diemates(c)) > 1 and diemates(c)[0] == c
 
     def by_switch(c):
         return [d for d in ranks if topo.same_plane(c, d)]
@@ -50,58 +53,61 @@ def rank_program(g, core, T, topo):
         return [d for d in ranks if topo.rack(topo.host(d)) != topo.rack(topo.host(c)) and topo.may_write(c, d)]
 
     def w_givers(c):
-        return by_cable(c) if crowded(c) else by_switch(c)
+        return by_cable(c) if cable_fed(c) else by_switch(c)
 
-    def partner(c):
-        return [d for d in (by_switch(c) if crowded(c) else by_cable(c)) if pos(d) == pos(c)][0]
+    def transfer(dst_cores, engines, sem, src, dst):
+        ids = [DstId(rid=topo.addr(d, core)[0], pnc=topo.addr(d, core)[1]) for d in dst_cores]
+        return RemoteDMATransfer(dst_ids=ids, dma_engine_mask=_bits(engines), remote_sem=sem,
+                                 srcs=[src], dsts=[dst for d in dst_cores])
 
-    def transfer(dst_core, engines, sem, src, dst):
-        rid, pid = topo.addr(dst_core, core)
-        return RemoteDMATransfer(dst_ids=[DstId(rid=rid, pnc=pid)], dma_engine_mask=_bits(engines), remote_sem=sem,
-                                 src=src, dst=dst)
-
-    mate = partner(core)
+    me = pos(core)
+    mate = [d for d in (by_switch(core) if cable_fed(core) else by_cable(core)) if pos(d) == me][0]
     near = [d for d in chipset(core) if d != core]
     off = _engines(topo.mask(core, mate))
     rest = [e for e in _engines(topo.mask(core, near[0])) if e not in off]
+    ev, od = off[0::2], off[1::2]
+    half = len(od) // 2
 
     g.sync.dma_start(T.wo[:], T.w[:]).then_inc(S.ld, 16)
     g.scalar.dma_start(T.xo[:], T.x[:]).then_inc(S.ld, 16)
 
-    far = []
-    for group in (by_switch(core), by_cable(core)):
-        for d in group:
-            if core in w_givers(d):
-                far.append((d, S["f%d" % pos(core)], T.wo[:], T.wf[:, pos(core) * D:(pos(core) + 1) * D]))
-            if d == mate:
-                far.append((d, S.xa, T.xo[:], T.xq[:]))
-    per = len(off) // len(far)
-    lanes = off[0::2] + off[1::2]
+    sw_d = [d for d in by_switch(core) if not cable_fed(d)]
+    cb_d = [d for d in by_cable(core) if cable_fed(d)]
+    turn = me % len(sw_d)
+    my_slot = T.wf[:, me * D:(me + 1) * D]
     g.wait_ge(S.ld, 32)
-    g.remote_dma_fused([transfer(d, lanes[i * per:(i + 1) * per], sem, src, dst)
-                        for i, (d, sem, src, dst) in enumerate(far)], local_sem=S.snd)
+    g.remote_dma_fused([transfer([mate], od[half:], S.xa, T.xo[:], T.xq[:]),
+                        transfer(cb_d, od[:half], S["f%d" % me], T.wo[:], my_slot),
+                        transfer(sw_d[turn:] + sw_d[:turn], ev, S["f%d" % me], T.wo[:], my_slot)],
+                       local_sem=S.snd)
     near_sorted = sorted(near, key=lambda d: topo.die(d) == topo.die(core))
     nper = len(rest) // len(near)
     nlanes = rest[0::2] + rest[1::2]
-    calls = []
+    near_t = []
     for i, d in enumerate(near_sorted):
         slot = [e for e in chipset(d) if e != d].index(core)
-        calls.append(transfer(d, nlanes[i * nper:(i + 1) * nper], S.cw, T.wo[:], T.wc[:, slot * D:(slot + 1) * D]))
-    g.remote_dma_fused(calls, local_sem=S.snd)
+        near_t.append(transfer([d], nlanes[i * nper:(i + 1) * nper], S.cw, T.wo[:], T.wc[:, slot * D:(slot + 1) * D]))
+    g.remote_dma_fused(near_t, local_sem=S.snd)
 
     te = g.tensor
     home = [T.wo[:], T.wc[:, 0:D], T.wc[:, D:2 * D]]
-    order = [pos(d) for d in sorted(w_givers(core), key=lambda d: (crowded(d), pos(d)))]
+    if cable_fed(core):
+        fin = half
+        order = [pos(d) for d in sorted(w_givers(core), key=lambda d: (len(diemates(d)), pos(d)))]
+    else:
+        fin = len(ev)
+        peers = [d for d in chipset(core) if not cable_fed(d)]
+        order = sorted(range(len(w_givers(core))), key=lambda k: ((peers.index(core) - k) % len(peers), k))
     te.wait_ge(S.ld, 32)
     te.matmul(T.p0[:, 0:D], home[0], T.xo[:], True, True).then_inc(S.m0, 1)
     te.wait_ge(S.cw, nper * len(near))
     for k in (1, 2):
         te.matmul(T.p0[:, k * D:(k + 1) * D], home[k], T.xo[:], True, True).then_inc(S.m0, 1)
-    te.wait_ge(S.xa, per)
+    te.wait_ge(S.xa, len(od) - half)
     for k in range(3):
         te.matmul(T["p%d" % (1 + k)][:, 0:D], home[k], T.xq[:], True, True).then_inc(S["m%d" % (1 + k)], 1)
     for k, j in enumerate(order):
-        te.wait_ge(S["f%d" % j], per)
+        te.wait_ge(S["f%d" % j], fin)
         te.matmul(T["p%d" % (4 + k)][:, 0:D], T.wf[:, j * D:(j + 1) * D], T.xq[:], True, True).then_inc(S["m%d" % (4 + k)], 1)
     for k, j in enumerate(order):
         te.matmul(T.p7[:, k * D:(k + 1) * D], T.wf[:, j * D:(j + 1) * D], T.xo[:], True, True).then_inc(S.m7, 1)
@@ -144,4 +150,4 @@ def rank_program(g, core, T, topo):
     g.sync.wait_ge(S.yd, 1)
     g.sync.dma_start(T.y[:], T.yb[:]).then_inc(S.st, 16)
     g.sync.wait_ge(S.st, 16)
-    g.wait_ge(S.snd, per * len(far) + nper * len(near) + len(off))
+    g.wait_ge(S.snd, len(off) + nper * len(near) + len(off))

from concourse.bass import DstId, RemoteDMATransfer
from concourse.mybir import AluOpType

D = 128

SCRATCH = {
    "wo": ("sbuf", [128, D], "bfloat16"),
    "xo": ("sbuf", [128, D], "bfloat16"),
    "wc": ("sbuf", [128, 2 * D], "bfloat16"),
    "wf": ("sbuf", [128, 3 * D], "bfloat16"),
    "xq": ("sbuf", [128, D], "bfloat16"),
    "ao": ("sbuf", [128, D], "bfloat16"),
    "aq": ("sbuf", [128, D], "bfloat16"),
    "rs": ("sbuf", [128, D], "bfloat16"),
    "yb": ("sbuf", [128, D], "bfloat16"),
}
for _b in range(8):
    SCRATCH["p%d" % _b] = ("psum", [128, 512], "float32")

SEMAPHORES = ["ld", "cw", "xa", "f0", "f1", "f2", "ra", "snd", "vs", "qd", "yd", "st"] + ["m%d" % _b for _b in range(8)]


def _engines(mask):
    return [e for e in range(mask.bit_length()) if (mask >> e) & 1]


def _bits(engines):
    return sum(1 << e for e in engines)


def rank_program(g, core, T, topo):
    if T.rank_of(core) is None:
        return
    S = T.sem
    ranks = list(T.cores)

    def chipset(c):
        return [d for d in ranks if topo.host(d) == topo.host(c) and topo.chip(d) == topo.chip(c)]

    def pos(c):
        return chipset(c).index(c)

    def diemates(c):
        return [d for d in chipset(c) if topo.die(d) == topo.die(c)]

    def cable_fed(c):
        return len(diemates(c)) > 1 and diemates(c)[0] == c

    def by_switch(c):
        return [d for d in ranks if topo.same_plane(c, d)]

    def by_cable(c):
        return [d for d in ranks if topo.rack(topo.host(d)) != topo.rack(topo.host(c)) and topo.may_write(c, d)]

    def w_givers(c):
        return by_cable(c) if cable_fed(c) else by_switch(c)

    def transfer(dst_cores, engines, sem, src, dst):
        ids = [DstId(rid=topo.addr(d, core)[0], pnc=topo.addr(d, core)[1]) for d in dst_cores]
        return RemoteDMATransfer(dst_ids=ids, dma_engine_mask=_bits(engines), remote_sem=sem,
                                 srcs=[src], dsts=[dst for d in dst_cores])

    me = pos(core)
    mate = [d for d in (by_switch(core) if cable_fed(core) else by_cable(core)) if pos(d) == me][0]
    near = [d for d in chipset(core) if d != core]
    off = _engines(topo.mask(core, mate))
    rest = [e for e in _engines(topo.mask(core, near[0])) if e not in off]
    ev, od = off[0::2], off[1::2]
    half = len(od) // 2

    g.sync.dma_start(T.wo[:], T.w[:]).then_inc(S.ld, 16)
    g.scalar.dma_start(T.xo[:], T.x[:]).then_inc(S.ld, 16)

    sw_d = [d for d in by_switch(core) if not cable_fed(d)]
    cb_d = [d for d in by_cable(core) if cable_fed(d)]
    turn = me % len(sw_d)
    my_slot = T.wf[:, me * D:(me + 1) * D]
    g.wait_ge(S.ld, 32)
    g.remote_dma_fused([transfer([mate], od[half:], S.xa, T.xo[:], T.xq[:]),
                        transfer(cb_d, od[:half], S["f%d" % me], T.wo[:], my_slot),
                        transfer(sw_d[turn:] + sw_d[:turn], ev, S["f%d" % me], T.wo[:], my_slot)],
                       local_sem=S.snd)
    near_sorted = sorted(near, key=lambda d: topo.die(d) == topo.die(core))
    nper = len(rest) // len(near)
    nlanes = rest[0::2] + rest[1::2]
    near_t = []
    for i, d in enumerate(near_sorted):
        slot = [e for e in chipset(d) if e != d].index(core)
        near_t.append(transfer([d], nlanes[i * nper:(i + 1) * nper], S.cw, T.wo[:], T.wc[:, slot * D:(slot + 1) * D]))
    g.remote_dma_fused(near_t, local_sem=S.snd)

    te = g.tensor
    home = [T.wo[:], T.wc[:, 0:D], T.wc[:, D:2 * D]]
    if cable_fed(core):
        fin = half
        order = [pos(d) for d in sorted(w_givers(core), key=lambda d: (len(diemates(d)), pos(d)))]
    else:
        fin = len(ev)
        peers = [d for d in chipset(core) if not cable_fed(d)]
        order = sorted(range(len(w_givers(core))), key=lambda k: ((peers.index(core) - k) % len(peers), k))
    te.wait_ge(S.ld, 32)
    te.matmul(T.p0[:, 0:D], home[0], T.xo[:], True, True).then_inc(S.m0, 1)
    te.wait_ge(S.cw, nper * len(near))
    for k in (1, 2):
        te.matmul(T.p0[:, k * D:(k + 1) * D], home[k], T.xo[:], True, True).then_inc(S.m0, 1)
    te.wait_ge(S.xa, len(od) - half)
    for k in range(3):
        te.matmul(T["p%d" % (1 + k)][:, 0:D], home[k], T.xq[:], True, True).then_inc(S["m%d" % (1 + k)], 1)
    for k, j in enumerate(order):
        te.wait_ge(S["f%d" % j], fin)
        te.matmul(T["p%d" % (4 + k)][:, 0:D], T.wf[:, j * D:(j + 1) * D], T.xq[:], True, True).then_inc(S["m%d" % (4 + k)], 1)
    for k, j in enumerate(order):
        te.matmul(T.p7[:, k * D:(k + 1) * D], T.wf[:, j * D:(j + 1) * D], T.xo[:], True, True).then_inc(S.m7, 1)

    ve = g.vector
    n = 0
    ve.wait_ge(S.m0, 3)
    ve.tensor_copy(T.ao[:], T.p0[:, 0:D]).then_inc(S.vs, 1)
    n += 1
    for k in (1, 2):
        ve.wait_ge(S.vs, n)
        ve.tensor_tensor(T.ao[:], T.ao[:], T.p0[:, k * D:(k + 1) * D], AluOpType.max).then_inc(S.vs, 1)
        n += 1
    ve.wait_ge(S.m1, 1)
    ve.tensor_copy(T.aq[:], T.p1[:, 0:D]).then_inc(S.vs, 1)
    n += 1
    for b in range(2, 7):
        ve.wait_ge(S["m%d" % b], 1)
        ve.wait_ge(S.vs, n)
        op = ve.tensor_tensor(T.aq[:], T.aq[:], T["p%d" % b][:, 0:D], AluOpType.max)
        if b < 6:
            op.then_inc(S.vs, 1)
            n += 1
        else:
            op.then_inc(S.qd, 1)
    ve.wait_ge(S.m7, 3)
    for k in range(3):
        ve.wait_ge(S.vs, n)
        out = T.ao[:] if k < 2 else T.p0[:, 0:D]
        ve.tensor_tensor(out, T.ao[:], T.p7[:, k * D:(k + 1) * D], AluOpType.max).then_inc(S.vs, 1)
        n += 1
    ve.wait_ge(S.ra, len(off))
    ve.wait_ge(S.vs, n)
    ve.tensor_tensor(T.yb[:], T.rs[:], T.p0[:, 0:D], AluOpType.max).then_inc(S.yd, 1)

    rid, pid = topo.addr(mate, core)
    g.wait_ge(S.qd, 1)
    g.remote_dma(T.rs[:], T.aq[:], S.ra, S.snd, pid, rid, _bits(off))

    g.sync.wait_ge(S.yd, 1)
    g.sync.dma_start(T.y[:], T.yb[:]).then_inc(S.st, 16)
    g.sync.wait_ge(S.st, 16)
    g.wait_ge(S.snd, len(off) + nper * len(near) + len(off))
